import numpy as np
import ml_dtypes


def mxq(x, axis, fmt="e4m3"):
    dtype, down = {"e4m3": (ml_dtypes.float8_e4m3fn, 7), "e5m2": (ml_dtypes.float8_e5m2, 14)}[fmt]
    v = np.moveaxis(np.asarray(x, np.float32).astype(ml_dtypes.bfloat16).astype(np.float64), axis, -1)
    blocks = v.reshape(v.shape[:-1] + (-1, 32))
    amax = np.abs(blocks).max(-1, keepdims=True)
    byte = np.maximum(np.where(amax > 0, np.frexp(amax)[1] - 1 + 127, 0) - down, 1)
    scale = np.exp2(byte - 127.0)
    codes = (blocks / scale).astype(np.float32).astype(dtype).astype(np.float64)
    return np.moveaxis((codes * scale).reshape(v.shape), -1, axis)


WIDE = False


def mx_kscale(k):
    if not WIDE:
        return np.ones(k)
    levels = np.array([10, -10, 5, -5, 0])
    if k % 512:
        return np.exp2(np.random.permutation(np.resize(levels, k // 32))).repeat(32)
    a = np.empty((k // 512, 16))
    for p in range(k // 512):
        a[p, :8] = np.random.permutation(np.resize(levels, 8))
        for g in range(8):
            far = levels[np.abs(levels - a[p, g]) >= 10]
            a[p, g + 8] = far[np.random.randint(len(far))]
    return np.exp2(a.ravel()).repeat(32)


def f64(x):
    return np.asarray(x).astype(np.float64)


def striped(idx):
    return np.tile(idx.reshape(-1, 16).T, (8, 1)).astype(np.uint16)


def unstriped(offs):
    return offs[:16].T.reshape(-1).astype(np.int64)


def pack_weight(w):
    k, n = w.shape
    w = f64(np.asarray(w, np.float32).astype(ml_dtypes.bfloat16)).reshape(k // 32, 32, n)
    amax = np.abs(w).max(1)
    byte = np.clip(np.where(amax > 0, np.frexp(amax)[1] - 1 + 127 - 7, 1), 1, 254)
    scaled = (w * np.exp2(127.0 - byte)[:, None, :]).reshape(k, n).astype(np.float32)
    words = np.ascontiguousarray(scaled.reshape(k // 512, 128, 4, n).transpose(0, 1, 3, 2)).astype(ml_dtypes.float8_e4m3fn).view(np.uint8)
    return words, np.ascontiguousarray(byte.astype(np.uint8).reshape(k // 512, 16, n))


def unpack_weight(words, scales):
    g, p, n, _ = words.shape
    vals = np.ascontiguousarray(words).view(ml_dtypes.float8_e4m3fn).astype(np.float64) * np.repeat(np.exp2(scales.astype(np.float64) - 127.0), 8, axis=1)[..., None]
    return vals.transpose(0, 1, 3, 2).reshape(g * 512, n)


def sigmoid(v):
    return 1.0 / (1.0 + np.exp(-np.maximum(v, -700.0)))


K, T, S, D, N, H, V, U = 512, 2048, 512, 2, 128, 512, 256, 512


def setup_inputs():
    n = np.random.standard_normal
    s = mx_kscale(K)[:, None]
    u = mx_kscale(H)
    packed_xT = pack_weight(n((K, T)) * s)
    return {
        "x_words": packed_xT[0],
        "x_scales": packed_xT[1],
        "w1": (n((K, H)) / np.sqrt(K) / s).astype(np.float32),
        "w2": (n((K, H)) / np.sqrt(K) / s).astype(np.float32),
        "st": (n((H, U))).astype(np.float32),
        "lam": (np.random.uniform(0.2, 1.0, (H, U))).astype(np.float32),
        "unit": (np.random.uniform(0.6, 1.4, (H, 1)) * u[:, None]).astype(np.float32),
        "w3": (n((H, N)) / np.sqrt(H) / u[:, None]).astype(np.float32),
        "offs": striped(np.random.permutation(T)[:S]),
        "m1": striped(np.random.permutation(np.concatenate([np.arange(V), np.random.randint(0, V, U - V)]))),
        "m2": striped(np.random.randint(0, U, U)),
    }


def reference(x_words, x_scales, w1, w2, st, lam, unit, w3, offs, m1, m2):
    xq = unpack_weight(x_words, x_scales)[:, unstriped(offs)]
    y = mxq(f64(w1), 0, "e4m3").T @ xq
    yg = mxq(f64(w2), 0, "e4m3").T @ xq
    ygt = y * sigmoid(yg)
    lv1 = ygt.reshape(len(ygt), -1, D).sum(axis=2)
    lm = lv1[:, unstriped(m1)]
    lv2 = lm + f64(st)
    lw = lv2 * f64(lam)
    hid = f64(unit) * (lw + lv2[:, unstriped(m2)])
    return mxq(f64(w3), 0, "e4m3").T @ mxq(hid, 0, "e4m3")

@@ -1,0 +1,252 @@
+from contextlib import ExitStack
+
+import concourse.mybir as mybir
+from concourse.masks import make_identity
+
+F32 = mybir.dt.float32
+BF16 = mybir.dt.bfloat16
+I32 = mybir.dt.int32
+U32 = mybir.dt.uint32
+U16 = mybir.dt.uint16
+U8 = mybir.dt.uint8
+FP8X4 = mybir.dt.float8_e4m3fn_x4
+ADD = mybir.AluOpType.add
+MULT = mybir.AluOpType.mult
+COPY = mybir.ActivationFunctionType.Copy
+SIGMOID = mybir.ActivationFunctionType.Sigmoid
+
+P = 128
+K, T, S, N, H, V, U = 512, 2048, 512, 128, 512, 256, 512
+PACK = 4
+RUN = 8
+CHUNKS = (256, 128, 128)
+
+FLOPS = 2 * K * H * S * 2 + 2 * H * N * U
+
+
+def tile_picked_yfenw_add_p_kernel(
+    tc, x_words, x_scales, w1, w2, st, lam, unit, w3, offs, m1, m2, out
+):
+    nc = tc.nc
+    with ExitStack() as ctx:
+        keep = ctx.enter_context(tc.tile_pool(name="keep", bufs=1))
+        psum = ctx.enter_context(tc.psum_pool(name="psum", bufs=1))
+
+        def tile(shape, dtype, name):
+            return keep.tile(shape, dtype, name=name, align_bytes=64)
+
+        def dealt_rows(src, t):
+            return src.rearrange("(b t r) c -> t b r c", t=PACK, r=RUN)[t]
+
+        offs_sb = keep.tile([P, S // 16], U16, name="offs_sb")
+        m1_sb = keep.tile([P, U // 16], U16, name="m1_sb")
+        m2_sb = keep.tile([P, U // 16], U16, name="m2_sb")
+        xw = tile([P, T], I32, "xw")
+        xs = tile([P, T], U8, "xs")
+        w_raw = [tile([P, PACK, H], F32, "w_raw%d" % i) for i in range(2)]
+        unit_rows = tile([P, P], F32, "unit_rows")
+        unit_sb = tile([P, PACK], F32, "unit_sb")
+        st_sb = [tile([P, U], F32, "st%d" % t) for t in range(PACK)]
+        lam_sb = [tile([P, U], F32, "lam%d" % t) for t in range(PACK)]
+        w3_raw = tile([P, PACK, N], F32, "w3_raw")
+
+        nc.vector.memset(xs[:].bitcast(I32), 0)
+        nc.vector.memset(unit_rows[:], 0.0)
+        nc.sync.dma_start(offs_sb[:], offs)
+        nc.sync.dma_start(xw[:], x_words[0].rearrange("p c r -> p (c r)").bitcast(I32))
+        for q in range(4):
+            nc.scalar.dma_start(xs[32 * q : 32 * q + 4, :].bitcast(I32), x_scales[0, 4 * q : 4 * q + 4, :].bitcast(I32))
+        nc.sync.dma_start(w_raw[1][:], w2.rearrange("(p j) c -> p j c", j=PACK))
+        nc.sync.dma_start(w_raw[0][:], w1.rearrange("(p j) c -> p j c", j=PACK))
+        nc.scalar.dma_start(unit_rows[0:PACK, :], unit.rearrange("(b t r) o -> t b (r o)", t=PACK, r=RUN))
+        nc.sync.dma_start(m1_sb[:], m1)
+        nc.sync.dma_start(st_sb[0][:], dealt_rows(st, 0))
+        for t in range(PACK):
+            if t + 1 < PACK:
+                nc.sync.dma_start(st_sb[t + 1][:], dealt_rows(st, t + 1))
+            nc.sync.dma_start(lam_sb[t][:], dealt_rows(lam, t))
+            if t == 0:
+                nc.sync.dma_start(m2_sb[:], m2)
+        for t in range(PACK):
+            nc.sync.dma_start(w3_raw[:, t, :], dealt_rows(w3, t))
+
+        warm = tile([P, 1], F32, "warm")
+        ident = tile([P, P], F32, "ident")
+        make_identity(nc, ident[:])
+        nc.scalar.activation(warm[:], ident[:, 0:1], SIGMOID)
+
+        ub = psum.tile([P, P], F32, name="ub", tag="lv", bufs=2)
+        nc.tensor.transpose(ub[:], unit_rows[:], ident[:])
+        nc.scalar.copy(unit_sb[:], ub[:, 0:PACK])
+
+        gb = tile([P, S], U8, "gb")
+        gbd = tile([P, S], U8, "gbd")
+        gw = tile([P, S], U32, "gw")
+        nc.vector.tensor_copy(gb[:], xs[:].indirect(offs_sb[:]))
+        nc.vector.tensor_copy(gw[:].rearrange("p (d v) -> p v d", d=2), xw[:].bitcast(U32).indirect(offs_sb[:]))
+        nc.vector.tensor_copy(gbd[:].rearrange("p (d v) -> p d v", d=2), gb[:].rearrange("p (v d) -> p d v", d=2))
+
+        wb = [[tile([P, P * PACK], BF16, "wb%d_%d" % (i, t)) for t in range(PACK)] for i in range(2)]
+        wq = [[tile([P, P], U32, "wq%d_%d" % (i, t)) for t in range(PACK)] for i in range(2)]
+        ws = [[tile([P, P], U8, "ws%d_%d" % (i, t)) for t in range(PACK)] for i in range(2)]
+
+        def weave_w(i, t, on_vector):
+            dst = wb[i][t][:].rearrange("p (b r j) -> p b j r", r=RUN, j=PACK)
+            src = w_raw[i][:].rearrange("p j (b t r) -> p t b j r", t=PACK, r=RUN)[:, t]
+            if on_vector:
+                nc.vector.tensor_copy(dst, src)
+            else:
+                nc.scalar.copy(dst, src)
+
+        def quant_w(i, t):
+            nc.vector.quantize_mx(out=wq[i][t][:].bitcast(FP8X4), scales=ws[i][t][:], in_=wb[i][t][:])
+
+        def product(i, t, tag, bufs):
+            bank = psum.tile([P, 4, P], F32, name="bank_%s" % tag, tag=tag, bufs=bufs)
+            for a in range(4):
+                cols = slice(a * P, (a + 1) * P)
+                nc.tensor.matmul_mx(
+                    out=bank[:, a, :], lhsT=gw[:, cols].bitcast(FP8X4), lhsT_scale=gbd[:, cols],
+                    rhs=wq[i][t][:].bitcast(FP8X4), rhs_scale=ws[i][t][:], start=True, stop=True,
+                )
+            return bank
+
+        win = [tile([P, V + S], F32, "win%d" % t) for t in range(PACK)]
+        ygt = [tile([P, S], F32, "ygt%d" % t) for t in range(PACK)]
+        stu = [tile([P, U], F32, "stu%d" % t) for t in range(PACK)]
+        lv2 = [tile([P, U], F32, "lv2_%d" % t) for t in range(PACK)]
+        lw = [tile([P, U], F32, "lw%d" % t) for t in range(PACK)]
+        ybank = {}
+        gbank = {}
+
+        def gate_product(t):
+            gbank[t] = product(1, t, "g", 3)
+
+        def gate(t):
+            nc.scalar.activation(win[t][:, V:], gbank[t][:].rearrange("p a f -> p (a f)"), SIGMOID)
+
+        def value_product(t):
+            ybank[t] = product(0, t, "y", 3)
+
+        def gated(t):
+            nc.vector.tensor_tensor(ygt[t][:], ybank[t][:].rearrange("p a f -> p (a f)"), win[t][:, V:], MULT)
+
+        def pair_sum(t):
+            lvb = psum.tile([P, V], F32, name="lvb", tag="lv", bufs=2)
+            for h in range(2):
+                for d in range(2):
+                    a = 2 * d + h
+                    nc.tensor.matmul(
+                        lvb[:, h * P : (h + 1) * P], lhsT=ygt[t][:, a * P : (a + 1) * P], rhs=ident[:],
+                        is_transpose=True, start=(d == 0), stop=(d == 1),
+                    )
+            nc.scalar.activation(win[t][:, 0:V], lvb[:], COPY, scale=unit_sb[:, t : t + 1])
+
+        def scale_st(t):
+            nc.scalar.activation(stu[t][:], st_sb[t][:], COPY, scale=unit_sb[:, t : t + 1])
+
+        def look_up_pairs(t):
+            nc.vector.tensor_tensor(lv2[t][:], win[t][:].indirect(m1_sb[:]), stu[t][:], ADD)
+
+        def weigh(t):
+            nc.vector.tensor_tensor(lw[t][:], lv2[t][:], lam_sb[t][:], MULT)
+
+        starts = [sum(CHUNKS[:c]) for c in range(len(CHUNKS))]
+        hid = [tile([P, PACK, w], F32, "hid%d" % c) for c, w in enumerate(CHUNKS)]
+        hb = [tile([P, PACK * w], BF16, "hb%d" % c) for c, w in enumerate(CHUNKS)]
+        hq = [tile([P, w], U32, "hq%d" % c) for c, w in enumerate(CHUNKS)]
+        hs = [tile([P, w], U8, "hs%d" % c) for c, w in enumerate(CHUNKS)]
+        res = [tile([P, w], F32, "res%d" % c) for c, w in enumerate(CHUNKS)]
+
+        def look_up_nodes(c, t):
+            c0, w = starts[c], CHUNKS[c]
+            nc.vector.tensor_tensor(
+                hid[c][:, t, :], lv2[t][:].indirect(m2_sb[:, c0 // 16 : (c0 + w) // 16]), lw[t][:, c0 : c0 + w], ADD
+            )
+
+        def weave_h(c, on_vector):
+            dst = hb[c][:].rearrange("p (g i t) -> p g t i", i=4, t=PACK)
+            src = hid[c][:].rearrange("p t (g i) -> p g t i", i=4)
+            if on_vector:
+                nc.vector.tensor_copy(dst, src)
+            else:
+                nc.scalar.copy(dst, src)
+
+        def finish(c):
+            c0, w = starts[c], CHUNKS[c]
+            nc.vector.quantize_mx(out=hq[c][:].bitcast(FP8X4), scales=hs[c][:], in_=hb[c][:])
+            ob = psum.tile([P, w], F32, name="ob", tag="g", bufs=3)
+            nc.tensor.matmul_mx(
+                out=ob[:], lhsT=w3q[:].bitcast(FP8X4), lhsT_scale=w3s[:],
+                rhs=hq[c][:].bitcast(FP8X4), rhs_scale=hs[c][:], start=True, stop=True,
+            )
+            nc.scalar.copy(res[c][:], ob[:])
+            nc.sync.dma_start(out[:, c0 : c0 + w], res[c][:])
+
+        weave_w(1, 0, True)
+        weave_w(1, 2, False)
+        weave_w(1, 1, True)
+        weave_w(1, 3, False)
+        for t in range(PACK):
+            quant_w(1, t)
+        gate_product(0)
+        gate_product(1)
+        gate_product(2)
+        gate(0)
+        gate(1)
+        gate_product(3)
+        weave_w(0, 0, True)
+        weave_w(0, 1, True)
+        quant_w(0, 0)
+        quant_w(0, 1)
+        weave_w(0, 2, False)
+        weave_w(0, 3, False)
+        value_product(0)
+        value_product(1)
+        gated(0)
+        gated(1)
+        scale_st(0)
+        pair_sum(0)
+        quant_w(0, 2)
+        quant_w(0, 3)
+        value_product(2)
+        gate(2)
+        scale_st(1)
+        pair_sum(1)
+        look_up_pairs(0)
+        value_product(3)
+        gate(3)
+        gated(2)
+        scale_st(2)
+        pair_sum(2)
+        look_up_pairs(1)
+        gated(3)
+        scale_st(3)
+        pair_sum(3)
+        weigh(0)
+        look_up_pairs(2)
+        weigh(1)
+        look_up_pairs(3)
+        weigh(2)
+
+        w3b = tile([P, N * PACK], BF16, "w3b")
+        w3q = tile([P, N], U32, "w3q")
+        w3s = tile([P, N], U8, "w3s")
+        nc.scalar.copy(
+            w3b[:].rearrange("p (g i t) -> p g t i", i=4, t=PACK), w3_raw[:].rearrange("p t (g i) -> p g t i", i=4)
+        )
+        look_up_nodes(0, 0)
+        weigh(3)
+        nc.vector.quantize_mx(out=w3q[:].bitcast(FP8X4), scales=w3s[:], in_=w3b[:])
+        for t in range(1, PACK):
+            look_up_nodes(0, t)
+        weave_h(0, False)
+        for t in range(PACK):
+            look_up_nodes(1, t)
+        weave_h(1, False)
+        for t in range(PACK):
+            look_up_nodes(2, t)
+        finish(0)
+        weave_h(2, True)
+        finish(1)
+        finish(2)

@@ -32,8 +32,8 @@ def tile_picked_yfenw_add_p_kernel(
         keep = ctx.enter_context(tc.tile_pool(name="keep", bufs=1))
         psum = ctx.enter_context(tc.psum_pool(name="psum", bufs=1))
 
-        def tile(shape, dtype, name):
-            return keep.tile(shape, dtype, name=name, align_bytes=64)
+        def tile(shape, dtype, name, on=None):
+            return keep.tile(shape, dtype, name=name, tag=on or name, align_bytes=64)
 
         def dealt_rows(src, t):
             return src.rearrange("(b t r) c -> t b r c", t=PACK, r=RUN)[t]
@@ -50,15 +50,17 @@ def tile_picked_yfenw_add_p_kernel(
         lam_sb = [tile([P, U], F32, "lam%d" % t) for t in range(PACK)]
         w3_raw = tile([P, PACK, N], F32, "w3_raw")
 
-        nc.vector.memset(xs[:].bitcast(I32), 0)
+        nc.gpsimd.memset(xs[:].bitcast(I32), 0)
         nc.vector.memset(unit_rows[:], 0.0)
-        nc.sync.dma_start(offs_sb[:], offs)
-        nc.sync.dma_start(xw[:], x_words[0].rearrange("p c r -> p (c r)").bitcast(I32))
+        w2_rows = w2.rearrange("(p j) c -> p j c", j=PACK)
+        nc.sync.dma_start(w_raw[1][:, 0:2, :], w2_rows[:, 0:2, :])
         for q in range(4):
-            nc.scalar.dma_start(xs[32 * q : 32 * q + 4, :].bitcast(I32), x_scales[0, 4 * q : 4 * q + 4, :].bitcast(I32))
-        nc.sync.dma_start(w_raw[1][:], w2.rearrange("(p j) c -> p j c", j=PACK))
+            nc.sync.dma_start(xs[32 * q : 32 * q + 4, :].bitcast(I32), x_scales[0, 4 * q : 4 * q + 4, :].bitcast(I32))
+        nc.sync.dma_start(offs_sb[:], offs)
+        nc.sync.dma_start(w_raw[1][:, 2:4, :], w2_rows[:, 2:4, :])
+        nc.sync.dma_start(xw[:], x_words[0].rearrange("p c r -> p (c r)").bitcast(I32))
         nc.sync.dma_start(w_raw[0][:], w1.rearrange("(p j) c -> p j c", j=PACK))
-        nc.scalar.dma_start(unit_rows[0:PACK, :], unit.rearrange("(b t r) o -> t b (r o)", t=PACK, r=RUN))
+        nc.sync.dma_start(unit_rows[0:PACK, :], unit.rearrange("(b t r) o -> t b (r o)", t=PACK, r=RUN))
         nc.sync.dma_start(m1_sb[:], m1)
         nc.sync.dma_start(st_sb[0][:], dealt_rows(st, 0))
         for t in range(PACK):
@@ -72,26 +74,25 @@ def tile_picked_yfenw_add_p_kernel(
 
         warm = tile([P, 1], F32, "warm")
         ident = tile([P, P], F32, "ident")
-        make_identity(nc, ident[:])
+        nc.gpsimd.memset(ident[:], 0.0)
         nc.scalar.activation(warm[:], ident[:, 0:1], SIGMOID)
+        make_identity(nc, ident[:], nomemset=True)
 
-        ub = psum.tile([P, P], F32, name="ub", tag="lv", bufs=2)
-        nc.tensor.transpose(ub[:], unit_rows[:], ident[:])
-        nc.scalar.copy(unit_sb[:], ub[:, 0:PACK])
 
         gb = tile([P, S], U8, "gb")
         gbd = tile([P, S], U8, "gbd")
         gw = tile([P, S], U32, "gw")
         nc.vector.tensor_copy(gb[:], xs[:].indirect(offs_sb[:]))
-        nc.vector.tensor_copy(gw[:].rearrange("p (d v) -> p v d", d=2), xw[:].bitcast(U32).indirect(offs_sb[:]))
         nc.vector.tensor_copy(gbd[:].rearrange("p (d v) -> p d v", d=2), gb[:].rearrange("p (v d) -> p d v", d=2))
 
-        wb = [[tile([P, P * PACK], BF16, "wb%d_%d" % (i, t)) for t in range(PACK)] for i in range(2)]
+        wb = {}
+        wb_on = {(0, 0): "wq1_0", (0, 1): "wq1_1", (0, 2): "wq1_3", (0, 3): "wq1_0"}
         wq = [[tile([P, P], U32, "wq%d_%d" % (i, t)) for t in range(PACK)] for i in range(2)]
         ws = [[tile([P, P], U8, "ws%d_%d" % (i, t)) for t in range(PACK)] for i in range(2)]
 
         def weave_w(i, t, on_vector):
-            dst = wb[i][t][:].rearrange("p (b r j) -> p b j r", r=RUN, j=PACK)
+            wb[i, t] = tile([P, P * PACK], BF16, "wb%d_%d" % (i, t), wb_on.get((i, t)))
+            dst = wb[i, t][:].rearrange("p (b r j) -> p b j r", r=RUN, j=PACK)
             src = w_raw[i][:].rearrange("p j (b t r) -> p t b j r", t=PACK, r=RUN)[:, t]
             if on_vector:
                 nc.vector.tensor_copy(dst, src)
@@ -99,7 +100,7 @@ def tile_picked_yfenw_add_p_kernel(
                 nc.scalar.copy(dst, src)
 
         def quant_w(i, t):
-            nc.vector.quantize_mx(out=wq[i][t][:].bitcast(FP8X4), scales=ws[i][t][:], in_=wb[i][t][:])
+            nc.vector.quantize_mx(out=wq[i][t][:].bitcast(FP8X4), scales=ws[i][t][:], in_=wb[i, t][:])
 
         def product(i, t, tag, bufs):
             bank = psum.tile([P, 4, P], F32, name="bank_%s" % tag, tag=tag, bufs=bufs)
@@ -113,7 +114,8 @@ def tile_picked_yfenw_add_p_kernel(
 
         win = [tile([P, V + S], F32, "win%d" % t) for t in range(PACK)]
         ygt = [tile([P, S], F32, "ygt%d" % t) for t in range(PACK)]
-        stu = [tile([P, U], F32, "stu%d" % t) for t in range(PACK)]
+        stu = {}
+        stu_on = ("wq1_1", "wq1_3", "ygt1", "ygt2")
         lv2 = [tile([P, U], F32, "lv2_%d" % t) for t in range(PACK)]
         lw = [tile([P, U], F32, "lw%d" % t) for t in range(PACK)]
         ybank = {}
@@ -143,6 +145,7 @@ def tile_picked_yfenw_add_p_kernel(
             nc.scalar.activation(win[t][:, 0:V], lvb[:], COPY, scale=unit_sb[:, t : t + 1])
 
         def scale_st(t):
+            stu[t] = tile([P, U], F32, "stu%d" % t, stu_on[t])
             nc.scalar.activation(stu[t][:], st_sb[t][:], COPY, scale=unit_sb[:, t : t + 1])
 
         def look_up_pairs(t):
@@ -152,7 +155,7 @@ def tile_picked_yfenw_add_p_kernel(
             nc.vector.tensor_tensor(lw[t][:], lv2[t][:], lam_sb[t][:], MULT)
 
         starts = [sum(CHUNKS[:c]) for c in range(len(CHUNKS))]
-        hid = [tile([P, PACK, w], F32, "hid%d" % c) for c, w in enumerate(CHUNKS)]
+        hid = {}
         hb = [tile([P, PACK * w], BF16, "hb%d" % c) for c, w in enumerate(CHUNKS)]
         hq = [tile([P, w], U32, "hq%d" % c) for c, w in enumerate(CHUNKS)]
         hs = [tile([P, w], U8, "hs%d" % c) for c, w in enumerate(CHUNKS)]
@@ -160,6 +163,8 @@ def tile_picked_yfenw_add_p_kernel(
 
         def look_up_nodes(c, t):
             c0, w = starts[c], CHUNKS[c]
+            if t == 0:
+                hid[c] = keep.tile([P, PACK, w], F32, name="hid", tag="hid%d" % (c % 2), align_bytes=64)
             nc.vector.tensor_tensor(
                 hid[c][:, t, :], lv2[t][:].indirect(m2_sb[:, c0 // 16 : (c0 + w) // 16]), lw[t][:, c0 : c0 + w], ADD
             )
@@ -180,7 +185,10 @@ def tile_picked_yfenw_add_p_kernel(
                 out=ob[:], lhsT=w3q[:].bitcast(FP8X4), lhsT_scale=w3s[:],
                 rhs=hq[c][:].bitcast(FP8X4), rhs_scale=hs[c][:], start=True, stop=True,
             )
-            nc.scalar.copy(res[c][:], ob[:])
+            if c == len(CHUNKS) - 1:
+                nc.vector.tensor_copy(res[c][:], ob[:])
+            else:
+                nc.scalar.copy(res[c][:], ob[:])
             nc.sync.dma_start(out[:, c0 : c0 + w], res[c][:])
 
         weave_w(1, 0, True)
@@ -189,31 +197,35 @@ def tile_picked_yfenw_add_p_kernel(
         weave_w(1, 3, False)
         for t in range(PACK):
             quant_w(1, t)
+        nc.vector.tensor_copy(gw[:].rearrange("p (d v) -> p v d", d=2), xw[:].bitcast(U32).indirect(offs_sb[:]))
         gate_product(0)
         gate_product(1)
         gate_product(2)
         gate(0)
         gate(1)
-        gate_product(3)
         weave_w(0, 0, True)
         weave_w(0, 1, True)
         quant_w(0, 0)
         quant_w(0, 1)
-        weave_w(0, 2, False)
-        weave_w(0, 3, False)
         value_product(0)
         value_product(1)
+        gate_product(3)
+        ub = psum.tile([P, P], F32, name="ub", tag="g", bufs=3)
+        nc.tensor.transpose(ub[:], unit_rows[:], ident[:])
+        nc.scalar.copy(unit_sb[:], ub[:, 0:PACK])
+        weave_w(0, 2, False)
         gated(0)
         gated(1)
         scale_st(0)
+        gate(2)
         pair_sum(0)
         quant_w(0, 2)
-        quant_w(0, 3)
         value_product(2)
-        gate(2)
+        weave_w(0, 3, False)
         scale_st(1)
         pair_sum(1)
         look_up_pairs(0)
+        quant_w(0, 3)
         value_product(3)
         gate(3)
         gated(2)
@@ -229,7 +241,7 @@ def tile_picked_yfenw_add_p_kernel(
         look_up_pairs(3)
         weigh(2)
 
-        w3b = tile([P, N * PACK], BF16, "w3b")
+        w3b = tile([P, N * PACK], BF16, "w3b", "ygt3")
         w3q = tile([P, N], U32, "w3q")
         w3s = tile([P, N], U8, "w3s")
         nc.scalar.copy(
@@ -244,9 +256,9 @@ def tile_picked_yfenw_add_p_kernel(
         for t in range(PACK):
             look_up_nodes(1, t)
         weave_h(1, False)
+        finish(0)
         for t in range(PACK):
             look_up_nodes(2, t)
-        finish(0)
         weave_h(2, True)
         finish(1)
         finish(2)

@@ -19,7 +19,12 @@ P = 128
 K, T, S, N, H, V, U = 512, 2048, 512, 128, 512, 256, 512
 PACK = 4
 RUN = 8
+GROUPS = 4
+HALF = H // 2
+PART = HALF // PACK
+LIST_ROWS = 16
 CHUNKS = (256, 128, 128)
+GATE_BANKS, VALUE_BANKS, PAIR_BANKS = 3, 3, 2
 
 FLOPS = 2 * K * H * S * 2 + 2 * H * N * U
 
@@ -32,36 +37,44 @@ def tile_picked_yfenw_add_p_kernel(
         keep = ctx.enter_context(tc.tile_pool(name="keep", bufs=1))
         psum = ctx.enter_context(tc.psum_pool(name="psum", bufs=1))
 
-        def tile(shape, dtype, name, on=None):
-            return keep.tile(shape, dtype, name=name, tag=on or name, align_bytes=64)
+        def tile(shape, dtype, name, after=None):
+            return keep.tile(shape, dtype, name=name, tag=after or name, align_bytes=64)
 
         def dealt_rows(src, t):
             return src.rearrange("(b t r) c -> t b r c", t=PACK, r=RUN)[t]
 
-        offs_sb = keep.tile([P, S // 16], U16, name="offs_sb")
-        m1_sb = keep.tile([P, U // 16], U16, name="m1_sb")
-        m2_sb = keep.tile([P, U // 16], U16, name="m2_sb")
-        xw = tile([P, T], I32, "xw")
-        xs = tile([P, T], U8, "xs")
-        w_raw = [tile([P, PACK, H], F32, "w_raw%d" % i) for i in range(2)]
+        def load_half(raw, w, h):
+            rows = w.rearrange("(p j) c -> p j c", j=PACK)
+            nc.sync.dma_start(raw[:], rows[:, :, h * HALF : (h + 1) * HALF])
+
+        offs_sb = keep.tile([P, S // LIST_ROWS], U16, name="offs_sb")
+        m1_sb = keep.tile([P, U // LIST_ROWS], U16, name="m1_sb")
+        m2_sb = keep.tile([P, U // LIST_ROWS], U16, name="m2_sb")
+        table_words = tile([P, T], I32, "table_words")
+        table_scales = tile([P, T], U8, "table_scales")
+        w2_raw = [tile([P, PACK, HALF], F32, "w2_raw%d" % h) for h in range(2)]
+        w1_raw = [tile([P, PACK, HALF], F32, "w1_raw%d" % h) for h in range(2)]
         unit_rows = tile([P, P], F32, "unit_rows")
         unit_sb = tile([P, PACK], F32, "unit_sb")
         st_sb = [tile([P, U], F32, "st%d" % t) for t in range(PACK)]
         lam_sb = [tile([P, U], F32, "lam%d" % t) for t in range(PACK)]
         w3_raw = tile([P, PACK, N], F32, "w3_raw")
 
-        nc.gpsimd.memset(xs[:].bitcast(I32), 0)
+        nc.gpsimd.memset(table_scales[:].bitcast(I32), 0)
         nc.vector.memset(unit_rows[:], 0.0)
-        w2_rows = w2.rearrange("(p j) c -> p j c", j=PACK)
-        nc.sync.dma_start(w_raw[1][:, 0:2, :], w2_rows[:, 0:2, :])
-        for q in range(4):
-            nc.sync.dma_start(xs[32 * q : 32 * q + 4, :].bitcast(I32), x_scales[0, 4 * q : 4 * q + 4, :].bitcast(I32))
+
         nc.sync.dma_start(offs_sb[:], offs)
-        nc.sync.dma_start(w_raw[1][:, 2:4, :], w2_rows[:, 2:4, :])
-        nc.sync.dma_start(xw[:], x_words[0].rearrange("p c r -> p (c r)").bitcast(I32))
-        nc.sync.dma_start(w_raw[0][:], w1.rearrange("(p j) c -> p j c", j=PACK))
-        nc.sync.dma_start(unit_rows[0:PACK, :], unit.rearrange("(b t r) o -> t b (r o)", t=PACK, r=RUN))
+        nc.sync.dma_start(table_words[:], x_words[0].rearrange("p c r -> p (c r)").bitcast(I32))
+        for q in range(4):
+            nc.sync.dma_start(
+                table_scales[32 * q : 32 * q + 4, :].bitcast(I32), x_scales[0, 4 * q : 4 * q + 4, :].bitcast(I32)
+            )
         nc.sync.dma_start(m1_sb[:], m1)
+        load_half(w2_raw[0], w2, 0)
+        load_half(w2_raw[1], w2, 1)
+        load_half(w1_raw[0], w1, 0)
+        load_half(w1_raw[1], w1, 1)
+        nc.gpsimd.dma_start(unit_rows[0:PACK, :], unit.rearrange("(b t r) o -> t b (r o)", t=PACK, r=RUN))
         nc.sync.dma_start(st_sb[0][:], dealt_rows(st, 0))
         for t in range(PACK):
             if t + 1 < PACK:
@@ -72,193 +85,196 @@ def tile_picked_yfenw_add_p_kernel(
         for t in range(PACK):
             nc.sync.dma_start(w3_raw[:, t, :], dealt_rows(w3, t))
 
-        warm = tile([P, 1], F32, "warm")
         ident = tile([P, P], F32, "ident")
+        warm = tile([P, 1], F32, "warm")
         nc.gpsimd.memset(ident[:], 0.0)
         nc.scalar.activation(warm[:], ident[:, 0:1], SIGMOID)
         make_identity(nc, ident[:], nomemset=True)
 
+        words = tile([P, S], U32, "words")
+        picked_scales = tile([P, S], U8, "picked_scales")
+        scales = tile([P, S], U8, "scales")
+        nc.vector.tensor_copy(
+            words[:].rearrange("p (d v) -> p v d", d=2), table_words[:].bitcast(U32).indirect(offs_sb[:])
+        )
+        nc.vector.tensor_copy(picked_scales[:], table_scales[:].indirect(offs_sb[:]))
+        nc.vector.tensor_copy(
+            scales[:].rearrange("p (d v) -> p d v", d=2), picked_scales[:].rearrange("p (v d) -> p d v", d=2)
+        )
 
-        gb = tile([P, S], U8, "gb")
-        gbd = tile([P, S], U8, "gbd")
-        gw = tile([P, S], U32, "gw")
-        nc.vector.tensor_copy(gb[:], xs[:].indirect(offs_sb[:]))
-        nc.vector.tensor_copy(gbd[:].rearrange("p (d v) -> p d v", d=2), gb[:].rearrange("p (v d) -> p d v", d=2))
-
-        wb = {}
-        wb_on = {(0, 0): "wq1_0", (0, 1): "wq1_1", (0, 2): "wq1_3", (0, 3): "wq1_0"}
-        wq = [[tile([P, P], U32, "wq%d_%d" % (i, t)) for t in range(PACK)] for i in range(2)]
-        ws = [[tile([P, P], U8, "ws%d_%d" % (i, t)) for t in range(PACK)] for i in range(2)]
-
-        def weave_w(i, t, on_vector):
-            wb[i, t] = tile([P, P * PACK], BF16, "wb%d_%d" % (i, t), wb_on.get((i, t)))
-            dst = wb[i, t][:].rearrange("p (b r j) -> p b j r", r=RUN, j=PACK)
-            src = w_raw[i][:].rearrange("p j (b t r) -> p t b j r", t=PACK, r=RUN)[:, t]
+        def copy_on(on_vector, dst, src):
             if on_vector:
                 nc.vector.tensor_copy(dst, src)
             else:
                 nc.scalar.copy(dst, src)
 
-        def quant_w(i, t):
-            nc.vector.quantize_mx(out=wq[i][t][:].bitcast(FP8X4), scales=ws[i][t][:], in_=wb[i, t][:])
+        def weave_weights(raw, t0, nt, name, on_vector):
+            woven = tile([P, nt * PART * PACK], BF16, name)
+            dst = woven[:].rearrange("p (t b r j) -> p t b j r", t=nt, r=RUN, j=PACK)
+            src = raw[:].rearrange("p j (b t r) -> p t b j r", t=PACK, r=RUN)[:, t0 : t0 + nt]
+            copy_on(on_vector, dst, src)
+            return woven
 
-        def product(i, t, tag, bufs):
-            bank = psum.tile([P, 4, P], F32, name="bank_%s" % tag, tag=tag, bufs=bufs)
-            for a in range(4):
-                cols = slice(a * P, (a + 1) * P)
+        def quantise(woven, columns, name):
+            codes = tile([P, columns], U32, name + "_codes")
+            planes = tile([P, columns], U8, name + "_scales")
+            nc.vector.quantize_mx(out=codes[:].bitcast(FP8X4), scales=planes[:], in_=woven[:])
+            return codes, planes
+
+        def product(quantised, first, tag, bufs):
+            codes, planes = quantised
+            bank = psum.tile([P, GROUPS, P], F32, name="bank_" + tag, tag=tag, bufs=bufs)
+            for a in range(GROUPS):
+                tokens = slice(a * P, (a + 1) * P)
                 nc.tensor.matmul_mx(
-                    out=bank[:, a, :], lhsT=gw[:, cols].bitcast(FP8X4), lhsT_scale=gbd[:, cols],
-                    rhs=wq[i][t][:].bitcast(FP8X4), rhs_scale=ws[i][t][:], start=True, stop=True,
+                    out=bank[:, a, :],
+                    lhsT=words[:, tokens].bitcast(FP8X4),
+                    lhsT_scale=scales[:, tokens],
+                    rhs=codes[:, first : first + P].bitcast(FP8X4),
+                    rhs_scale=planes[:, first : first + P],
+                    start=True,
+                    stop=True,
                 )
             return bank
 
-        win = [tile([P, V + S], F32, "win%d" % t) for t in range(PACK)]
-        ygt = [tile([P, S], F32, "ygt%d" % t) for t in range(PACK)]
-        stu = {}
-        stu_on = ("wq1_1", "wq1_3", "ygt1", "ygt2")
+        window = [tile([P, V + S], F32, "window%d" % t) for t in range(PACK)]
+        gated = [tile([P, GROUPS, 2, 2, PART], F32, "gated%d" % u) for u in range(2)]
         lv2 = [tile([P, U], F32, "lv2_%d" % t) for t in range(PACK)]
         lw = [tile([P, U], F32, "lw%d" % t) for t in range(PACK)]
-        ybank = {}
-        gbank = {}
+        st_scaled = {}
+        st_scaled_after = (None, "gated0", "gated1", "st_scaled0")
 
-        def gate_product(t):
-            gbank[t] = product(1, t, "g", 3)
+        def sigmoids(h, u):
+            return window[2 * h + u][:, V:]
 
-        def gate(t):
-            nc.scalar.activation(win[t][:, V:], gbank[t][:].rearrange("p a f -> p (a f)"), SIGMOID)
+        def gate(h, u, bank):
+            nc.scalar.activation(sigmoids(h, u), bank[:].rearrange("p a f -> p (a f)"), SIGMOID)
 
-        def value_product(t):
-            ybank[t] = product(0, t, "y", 3)
-
-        def gated(t):
-            nc.vector.tensor_tensor(ygt[t][:], ybank[t][:].rearrange("p a f -> p (a f)"), win[t][:, V:], MULT)
+        def apply_gate(h, u, bank):
+            nc.vector.tensor_tensor(
+                gated[u][:, :, :, h, :].rearrange("p a t f -> p (a t) f"),
+                bank[:].rearrange("p a (t f) -> p (a t) f", t=2),
+                sigmoids(h, u).rearrange("p (g f) -> p g f", f=PART),
+                MULT,
+            )
 
         def pair_sum(t):
-            lvb = psum.tile([P, V], F32, name="lvb", tag="lv", bufs=2)
+            bank = psum.tile([P, V], F32, name="bank_pair", tag="pair", bufs=PAIR_BANKS)
             for h in range(2):
                 for d in range(2):
-                    a = 2 * d + h
                     nc.tensor.matmul(
-                        lvb[:, h * P : (h + 1) * P], lhsT=ygt[t][:, a * P : (a + 1) * P], rhs=ident[:],
-                        is_transpose=True, start=(d == 0), stop=(d == 1),
+                        bank[:, h * P : (h + 1) * P],
+                        lhsT=gated[t // 2][:, 2 * d + h, t % 2].rearrange("p h f -> p (h f)"),
+                        rhs=ident[:],
+                        is_transpose=True,
+                        start=(d == 0),
+                        stop=(d == 1),
                     )
-            nc.scalar.activation(win[t][:, 0:V], lvb[:], COPY, scale=unit_sb[:, t : t + 1])
+            nc.scalar.activation(window[t][:, 0:V], bank[:], COPY, scale=unit_sb[:, t : t + 1])
 
         def scale_st(t):
-            stu[t] = tile([P, U], F32, "stu%d" % t, stu_on[t])
-            nc.scalar.activation(stu[t][:], st_sb[t][:], COPY, scale=unit_sb[:, t : t + 1])
+            st_scaled[t] = tile([P, U], F32, "st_scaled%d" % t, st_scaled_after[t])
+            nc.scalar.activation(st_scaled[t][:], st_sb[t][:], COPY, scale=unit_sb[:, t : t + 1])
 
         def look_up_pairs(t):
-            nc.vector.tensor_tensor(lv2[t][:], win[t][:].indirect(m1_sb[:]), stu[t][:], ADD)
+            nc.vector.tensor_tensor(lv2[t][:], window[t][:].indirect(m1_sb[:]), st_scaled[t][:], ADD)
 
         def weigh(t):
             nc.vector.tensor_tensor(lw[t][:], lv2[t][:], lam_sb[t][:], MULT)
 
-        starts = [sum(CHUNKS[:c]) for c in range(len(CHUNKS))]
-        hid = {}
-        hb = [tile([P, PACK * w], BF16, "hb%d" % c) for c, w in enumerate(CHUNKS)]
-        hq = [tile([P, w], U32, "hq%d" % c) for c, w in enumerate(CHUNKS)]
-        hs = [tile([P, w], U8, "hs%d" % c) for c, w in enumerate(CHUNKS)]
-        res = [tile([P, w], F32, "res%d" % c) for c, w in enumerate(CHUNKS)]
+        w2q = []
+        for h in range(2):
+            w2q.append(quantise(weave_weights(w2_raw[h], 0, PACK, "w2_woven%d" % h, False), HALF, "w2_%d" % h))
+        gate_00 = product(w2q[0], 0, "gate", GATE_BANKS)
+        gate_01 = product(w2q[0], P, "gate", GATE_BANKS)
+        gate_10 = product(w2q[1], 0, "gate", GATE_BANKS)
+        gate(0, 0, gate_00)
+        gate_11 = product(w2q[1], P, "gate", GATE_BANKS)
+        gate(0, 1, gate_01)
+        gate(1, 0, gate_10)
+        gate(1, 1, gate_11)
+        unit_bank = psum.tile([P, P], F32, name="unit_bank", tag="gate", bufs=GATE_BANKS)
+        nc.tensor.transpose(unit_bank[:], unit_rows[:], ident[:])
+        nc.scalar.copy(unit_sb[:], unit_bank[:, 0:PACK])
 
-        def look_up_nodes(c, t):
-            c0, w = starts[c], CHUNKS[c]
-            if t == 0:
-                hid[c] = keep.tile([P, PACK, w], F32, name="hid", tag="hid%d" % (c % 2), align_bytes=64)
-            nc.vector.tensor_tensor(
-                hid[c][:, t, :], lv2[t][:].indirect(m2_sb[:, c0 // 16 : (c0 + w) // 16]), lw[t][:, c0 : c0 + w], ADD
-            )
-
-        def weave_h(c, on_vector):
-            dst = hb[c][:].rearrange("p (g i t) -> p g t i", i=4, t=PACK)
-            src = hid[c][:].rearrange("p t (g i) -> p g t i", i=4)
-            if on_vector:
-                nc.vector.tensor_copy(dst, src)
-            else:
-                nc.scalar.copy(dst, src)
-
-        def finish(c):
-            c0, w = starts[c], CHUNKS[c]
-            nc.vector.quantize_mx(out=hq[c][:].bitcast(FP8X4), scales=hs[c][:], in_=hb[c][:])
-            ob = psum.tile([P, w], F32, name="ob", tag="g", bufs=3)
-            nc.tensor.matmul_mx(
-                out=ob[:], lhsT=w3q[:].bitcast(FP8X4), lhsT_scale=w3s[:],
-                rhs=hq[c][:].bitcast(FP8X4), rhs_scale=hs[c][:], start=True, stop=True,
-            )
-            if c == len(CHUNKS) - 1:
-                nc.vector.tensor_copy(res[c][:], ob[:])
-            else:
-                nc.scalar.copy(res[c][:], ob[:])
-            nc.sync.dma_start(out[:, c0 : c0 + w], res[c][:])
-
-        weave_w(1, 0, True)
-        weave_w(1, 2, False)
-        weave_w(1, 1, True)
-        weave_w(1, 3, False)
-        for t in range(PACK):
-            quant_w(1, t)
-        nc.vector.tensor_copy(gw[:].rearrange("p (d v) -> p v d", d=2), xw[:].bitcast(U32).indirect(offs_sb[:]))
-        gate_product(0)
-        gate_product(1)
-        gate_product(2)
-        gate(0)
-        gate(1)
-        weave_w(0, 0, True)
-        weave_w(0, 1, True)
-        quant_w(0, 0)
-        quant_w(0, 1)
-        value_product(0)
-        value_product(1)
-        gate_product(3)
-        ub = psum.tile([P, P], F32, name="ub", tag="g", bufs=3)
-        nc.tensor.transpose(ub[:], unit_rows[:], ident[:])
-        nc.scalar.copy(unit_sb[:], ub[:, 0:PACK])
-        weave_w(0, 2, False)
-        gated(0)
-        gated(1)
+        w1q_0 = quantise(weave_weights(w1_raw[0], 0, PACK, "w1_woven0", True), HALF, "w1_0")
+        w1_woven10 = weave_weights(w1_raw[1], 0, 2, "w1_woven10", True)
+        w1_woven11 = weave_weights(w1_raw[1], 2, 2, "w1_woven11", False)
+        value_00 = product(w1q_0, 0, "value", VALUE_BANKS)
+        value_10 = product(quantise(w1_woven10, P, "w1_10"), 0, "value", VALUE_BANKS)
+        value_01 = product(w1q_0, P, "value", VALUE_BANKS)
+        apply_gate(0, 0, value_00)
+        apply_gate(1, 0, value_10)
         scale_st(0)
-        gate(2)
         pair_sum(0)
-        quant_w(0, 2)
-        value_product(2)
-        weave_w(0, 3, False)
-        scale_st(1)
+        value_11 = product(quantise(w1_woven11, P, "w1_11"), 0, "value", VALUE_BANKS)
+        apply_gate(0, 1, value_01)
         pair_sum(1)
+        apply_gate(1, 1, value_11)
+        scale_st(1)
         look_up_pairs(0)
-        quant_w(0, 3)
-        value_product(3)
-        gate(3)
-        gated(2)
-        scale_st(2)
         pair_sum(2)
-        look_up_pairs(1)
-        gated(3)
-        scale_st(3)
         pair_sum(3)
+        scale_st(2)
+        look_up_pairs(1)
+        scale_st(3)
         weigh(0)
         look_up_pairs(2)
         weigh(1)
         look_up_pairs(3)
         weigh(2)
 
-        w3b = tile([P, N * PACK], BF16, "w3b", "ygt3")
-        w3q = tile([P, N], U32, "w3q")
-        w3s = tile([P, N], U8, "w3s")
-        nc.scalar.copy(
-            w3b[:].rearrange("p (g i t) -> p g t i", i=4, t=PACK), w3_raw[:].rearrange("p t (g i) -> p g t i", i=4)
-        )
+        def weave_rows(dst, src, on_vector):
+            copy_on(
+                on_vector,
+                dst.rearrange("p (g i t) -> p g t i", i=4, t=PACK),
+                src.rearrange("p t (g i) -> p g t i", i=4),
+            )
+
+        w3_woven = tile([P, N * PACK], BF16, "w3_woven", "gated0")
+        weave_rows(w3_woven[:], w3_raw[:], False)
+
+        starts = [sum(CHUNKS[:c]) for c in range(len(CHUNKS))]
+        last = len(CHUNKS) - 1
+        hid = {}
+        hid_woven = [tile([P, PACK * width], BF16, "hid_woven%d" % c) for c, width in enumerate(CHUNKS)]
+
+        def look_up_nodes(c, t):
+            c0, width = starts[c], CHUNKS[c]
+            if t == 0:
+                hid[c] = tile([P, PACK, width], F32, "hid%d" % c, "hid%d" % (c % 2))
+            offsets = m2_sb[:, c0 // LIST_ROWS : (c0 + width) // LIST_ROWS]
+            nc.vector.tensor_tensor(hid[c][:, t, :], lv2[t][:].indirect(offsets), lw[t][:, c0 : c0 + width], ADD)
+
+        def project(c):
+            c0, width = starts[c], CHUNKS[c]
+            codes, planes = quantise(hid_woven[c], width, "hid_%d" % c)
+            bank = psum.tile([P, width], F32, name="bank_out", tag="gate", bufs=GATE_BANKS)
+            nc.tensor.matmul_mx(
+                out=bank[:],
+                lhsT=w3_codes[:].bitcast(FP8X4),
+                lhsT_scale=w3_scales[:],
+                rhs=codes[:].bitcast(FP8X4),
+                rhs_scale=planes[:],
+                start=True,
+                stop=True,
+            )
+            result = tile([P, width], F32, "result%d" % c)
+            copy_on(c == last, result[:], bank[:])
+            nc.sync.dma_start(out[:, c0 : c0 + width], result[:])
+
         look_up_nodes(0, 0)
         weigh(3)
-        nc.vector.quantize_mx(out=w3q[:].bitcast(FP8X4), scales=w3s[:], in_=w3b[:])
+        w3_codes, w3_scales = quantise(w3_woven, N, "w3")
         for t in range(1, PACK):
             look_up_nodes(0, t)
-        weave_h(0, False)
+        weave_rows(hid_woven[0][:], hid[0][:], False)
         for t in range(PACK):
             look_up_nodes(1, t)
-        weave_h(1, False)
-        finish(0)
+        weave_rows(hid_woven[1][:], hid[1][:], False)
+        project(0)
         for t in range(PACK):
             look_up_nodes(2, t)
-        weave_h(2, True)
-        finish(1)
-        finish(2)
+        weave_rows(hid_woven[2][:], hid[2][:], True)
+        project(1)
+        project(2)

@@ -20,8 +20,6 @@ K, T, S, N, H, V, U = 512, 2048, 512, 128, 512, 256, 512
 PACK = 4
 RUN = 8
 GROUPS = 4
-HALF = H // 2
-PART = HALF // PACK
 LIST_ROWS = 16
 CHUNKS = (256, 128, 128)
 GATE_BANKS, VALUE_BANKS, PAIR_BANKS = 3, 3, 2
@@ -43,17 +41,13 @@ def tile_picked_yfenw_add_p_kernel(
         def dealt_rows(src, t):
             return src.rearrange("(b t r) c -> t b r c", t=PACK, r=RUN)[t]
 
-        def load_half(raw, w, h):
-            rows = w.rearrange("(p j) c -> p j c", j=PACK)
-            nc.sync.dma_start(raw[:], rows[:, :, h * HALF : (h + 1) * HALF])
-
         offs_sb = keep.tile([P, S // LIST_ROWS], U16, name="offs_sb")
         m1_sb = keep.tile([P, U // LIST_ROWS], U16, name="m1_sb")
         m2_sb = keep.tile([P, U // LIST_ROWS], U16, name="m2_sb")
         table_words = tile([P, T], I32, "table_words")
         table_scales = tile([P, T], U8, "table_scales")
-        w2_raw = [tile([P, PACK, HALF], F32, "w2_raw%d" % h) for h in range(2)]
-        w1_raw = [tile([P, PACK, HALF], F32, "w1_raw%d" % h) for h in range(2)]
+        w2_raw = tile([P, PACK, H], F32, "w2_raw")
+        w1_raw = tile([P, PACK, H], F32, "w1_raw")
         unit_rows = tile([P, P], F32, "unit_rows")
         unit_sb = tile([P, PACK], F32, "unit_sb")
         st_sb = [tile([P, U], F32, "st%d" % t) for t in range(PACK)]
@@ -63,18 +57,18 @@ def tile_picked_yfenw_add_p_kernel(
         nc.gpsimd.memset(table_scales[:].bitcast(I32), 0)
         nc.vector.memset(unit_rows[:], 0.0)
 
-        nc.sync.dma_start(offs_sb[:], offs)
-        nc.sync.dma_start(table_words[:], x_words[0].rearrange("p c r -> p (c r)").bitcast(I32))
+        w2_rows = w2.rearrange("(p j) c -> p j c", j=PACK)
+        nc.sync.dma_start(w2_raw[:, 0:2, :], w2_rows[:, 0:2, :])
         for q in range(4):
             nc.sync.dma_start(
                 table_scales[32 * q : 32 * q + 4, :].bitcast(I32), x_scales[0, 4 * q : 4 * q + 4, :].bitcast(I32)
             )
+        nc.sync.dma_start(offs_sb[:], offs)
+        nc.sync.dma_start(table_words[:], x_words[0].rearrange("p c r -> p (c r)").bitcast(I32))
+        nc.sync.dma_start(w2_raw[:, 2:4, :], w2_rows[:, 2:4, :])
+        nc.sync.dma_start(w1_raw[:], w1.rearrange("(p j) c -> p j c", j=PACK))
+        nc.sync.dma_start(unit_rows[0:PACK, :], unit.rearrange("(b t r) o -> t b (r o)", t=PACK, r=RUN))
         nc.sync.dma_start(m1_sb[:], m1)
-        load_half(w2_raw[0], w2, 0)
-        load_half(w2_raw[1], w2, 1)
-        load_half(w1_raw[0], w1, 0)
-        load_half(w1_raw[1], w1, 1)
-        nc.gpsimd.dma_start(unit_rows[0:PACK, :], unit.rearrange("(b t r) o -> t b (r o)", t=PACK, r=RUN))
         nc.sync.dma_start(st_sb[0][:], dealt_rows(st, 0))
         for t in range(PACK):
             if t + 1 < PACK:
@@ -94,12 +88,12 @@ def tile_picked_yfenw_add_p_kernel(
         words = tile([P, S], U32, "words")
         picked_scales = tile([P, S], U8, "picked_scales")
         scales = tile([P, S], U8, "scales")
-        nc.vector.tensor_copy(
-            words[:].rearrange("p (d v) -> p v d", d=2), table_words[:].bitcast(U32).indirect(offs_sb[:])
-        )
         nc.vector.tensor_copy(picked_scales[:], table_scales[:].indirect(offs_sb[:]))
         nc.vector.tensor_copy(
             scales[:].rearrange("p (d v) -> p d v", d=2), picked_scales[:].rearrange("p (v d) -> p d v", d=2)
+        )
+        nc.vector.tensor_copy(
+            words[:].rearrange("p (d v) -> p v d", d=2), table_words[:].bitcast(U32).indirect(offs_sb[:])
         )
 
         def copy_on(on_vector, dst, src):
@@ -108,10 +102,10 @@ def tile_picked_yfenw_add_p_kernel(
             else:
                 nc.scalar.copy(dst, src)
 
-        def weave_weights(raw, t0, nt, name, on_vector):
-            woven = tile([P, nt * PART * PACK], BF16, name)
-            dst = woven[:].rearrange("p (t b r j) -> p t b j r", t=nt, r=RUN, j=PACK)
-            src = raw[:].rearrange("p j (b t r) -> p t b j r", t=PACK, r=RUN)[:, t0 : t0 + nt]
+        def weave_weights(raw, t, name, on_vector):
+            woven = tile([P, P * PACK], BF16, name)
+            dst = woven[:].rearrange("p (b r j) -> p b j r", r=RUN, j=PACK)
+            src = raw[:].rearrange("p j (b t r) -> p t b j r", t=PACK, r=RUN)[:, t]
             copy_on(on_vector, dst, src)
             return woven
 
@@ -121,7 +115,7 @@ def tile_picked_yfenw_add_p_kernel(
             nc.vector.quantize_mx(out=codes[:].bitcast(FP8X4), scales=planes[:], in_=woven[:])
             return codes, planes
 
-        def product(quantised, first, tag, bufs):
+        def product(quantised, tag, bufs):
             codes, planes = quantised
             bank = psum.tile([P, GROUPS, P], F32, name="bank_" + tag, tag=tag, bufs=bufs)
             for a in range(GROUPS):
@@ -130,32 +124,26 @@ def tile_picked_yfenw_add_p_kernel(
                     out=bank[:, a, :],
                     lhsT=words[:, tokens].bitcast(FP8X4),
                     lhsT_scale=scales[:, tokens],
-                    rhs=codes[:, first : first + P].bitcast(FP8X4),
-                    rhs_scale=planes[:, first : first + P],
+                    rhs=codes[:].bitcast(FP8X4),
+                    rhs_scale=planes[:],
                     start=True,
                     stop=True,
                 )
             return bank
 
         window = [tile([P, V + S], F32, "window%d" % t) for t in range(PACK)]
-        gated = [tile([P, GROUPS, 2, 2, PART], F32, "gated%d" % u) for u in range(2)]
+        gated = [tile([P, GROUPS, P], F32, "gated%d" % t) for t in range(PACK)]
         lv2 = [tile([P, U], F32, "lv2_%d" % t) for t in range(PACK)]
         lw = [tile([P, U], F32, "lw%d" % t) for t in range(PACK)]
         st_scaled = {}
-        st_scaled_after = (None, "gated0", "gated1", "st_scaled0")
+        st_scaled_after = (None, "gated0", "gated1", "gated2")
 
-        def sigmoids(h, u):
-            return window[2 * h + u][:, V:]
+        def gate(t, bank):
+            nc.scalar.activation(window[t][:, V:], bank[:].rearrange("p a f -> p (a f)"), SIGMOID)
 
-        def gate(h, u, bank):
-            nc.scalar.activation(sigmoids(h, u), bank[:].rearrange("p a f -> p (a f)"), SIGMOID)
-
-        def apply_gate(h, u, bank):
+        def apply_gate(t, bank):
             nc.vector.tensor_tensor(
-                gated[u][:, :, :, h, :].rearrange("p a t f -> p (a t) f"),
-                bank[:].rearrange("p a (t f) -> p (a t) f", t=2),
-                sigmoids(h, u).rearrange("p (g f) -> p g f", f=PART),
-                MULT,
+                gated[t][:].rearrange("p a f -> p (a f)"), bank[:].rearrange("p a f -> p (a f)"), window[t][:, V:], MULT
             )
 
         def pair_sum(t):
@@ -164,7 +152,7 @@ def tile_picked_yfenw_add_p_kernel(
                 for d in range(2):
                     nc.tensor.matmul(
                         bank[:, h * P : (h + 1) * P],
-                        lhsT=gated[t // 2][:, 2 * d + h, t % 2].rearrange("p h f -> p (h f)"),
+                        lhsT=gated[t][:, 2 * d + h, :],
                         rhs=ident[:],
                         is_transpose=True,
                         start=(d == 0),
@@ -182,41 +170,37 @@ def tile_picked_yfenw_add_p_kernel(
         def weigh(t):
             nc.vector.tensor_tensor(lw[t][:], lv2[t][:], lam_sb[t][:], MULT)
 
-        w2q = []
-        for h in range(2):
-            w2q.append(quantise(weave_weights(w2_raw[h], 0, PACK, "w2_woven%d" % h, False), HALF, "w2_%d" % h))
-        gate_00 = product(w2q[0], 0, "gate", GATE_BANKS)
-        gate_01 = product(w2q[0], P, "gate", GATE_BANKS)
-        gate_10 = product(w2q[1], 0, "gate", GATE_BANKS)
-        gate(0, 0, gate_00)
-        gate_11 = product(w2q[1], P, "gate", GATE_BANKS)
-        gate(0, 1, gate_01)
-        gate(1, 0, gate_10)
-        gate(1, 1, gate_11)
+        w2_woven = [weave_weights(w2_raw, t, "w2_woven%d" % t, t == PACK - 1) for t in range(PACK)]
+        w2q = [quantise(w2_woven[t], P, "w2_%d" % t) for t in range(PACK)]
+        gate_banks = [product(w2q[t], "gate", GATE_BANKS) for t in range(GATE_BANKS)]
+        gate(0, gate_banks[0])
+        gate_banks.append(product(w2q[3], "gate", GATE_BANKS))
+        for t in range(1, PACK):
+            gate(t, gate_banks[t])
         unit_bank = psum.tile([P, P], F32, name="unit_bank", tag="gate", bufs=GATE_BANKS)
         nc.tensor.transpose(unit_bank[:], unit_rows[:], ident[:])
         nc.scalar.copy(unit_sb[:], unit_bank[:, 0:PACK])
 
-        w1q_0 = quantise(weave_weights(w1_raw[0], 0, PACK, "w1_woven0", True), HALF, "w1_0")
-        w1_woven10 = weave_weights(w1_raw[1], 0, 2, "w1_woven10", True)
-        w1_woven11 = weave_weights(w1_raw[1], 2, 2, "w1_woven11", False)
-        value_00 = product(w1q_0, 0, "value", VALUE_BANKS)
-        value_10 = product(quantise(w1_woven10, P, "w1_10"), 0, "value", VALUE_BANKS)
-        value_01 = product(w1q_0, P, "value", VALUE_BANKS)
-        apply_gate(0, 0, value_00)
-        apply_gate(1, 0, value_10)
+        w1_woven = [weave_weights(w1_raw, t, "w1_woven%d" % t, True) for t in (0, 1)]
+        w1q = [quantise(w1_woven[t], P, "w1_%d" % t) for t in (0, 1)]
+        w1_woven.append(weave_weights(w1_raw, 2, "w1_woven2", False))
+        value_banks = [product(w1q[t], "value", VALUE_BANKS) for t in (0, 1)]
+        apply_gate(0, value_banks[0])
+        apply_gate(1, value_banks[1])
         scale_st(0)
         pair_sum(0)
-        value_11 = product(quantise(w1_woven11, P, "w1_11"), 0, "value", VALUE_BANKS)
-        apply_gate(0, 1, value_01)
+        value_banks.append(product(quantise(w1_woven[2], P, "w1_2"), "value", VALUE_BANKS))
+        w1_woven.append(weave_weights(w1_raw, 3, "w1_woven3", False))
         pair_sum(1)
-        apply_gate(1, 1, value_11)
         scale_st(1)
         look_up_pairs(0)
+        value_banks.append(product(quantise(w1_woven[3], P, "w1_3"), "value", VALUE_BANKS))
+        apply_gate(2, value_banks[2])
         pair_sum(2)
-        pair_sum(3)
         scale_st(2)
         look_up_pairs(1)
+        apply_gate(3, value_banks[3])
+        pair_sum(3)
         scale_st(3)
         weigh(0)
         look_up_pairs(2)
@@ -231,7 +215,7 @@ def tile_picked_yfenw_add_p_kernel(
                 src.rearrange("p t (g i) -> p g t i", i=4),
             )
 
-        w3_woven = tile([P, N * PACK], BF16, "w3_woven", "gated0")
+        w3_woven = tile([P, N * PACK], BF16, "w3_woven", "gated3")
         weave_rows(w3_woven[:], w3_raw[:], False)
 
         starts = [sum(CHUNKS[:c]) for c in range(len(CHUNKS))]

from contextlib import ExitStack

import concourse.mybir as mybir
from concourse.masks import make_identity

F32 = mybir.dt.float32
BF16 = mybir.dt.bfloat16
I32 = mybir.dt.int32
U32 = mybir.dt.uint32
U16 = mybir.dt.uint16
U8 = mybir.dt.uint8
FP8X4 = mybir.dt.float8_e4m3fn_x4
ADD = mybir.AluOpType.add
MULT = mybir.AluOpType.mult
COPY = mybir.ActivationFunctionType.Copy
SIGMOID = mybir.ActivationFunctionType.Sigmoid

P = 128
K, T, S, N, H, V, U = 512, 2048, 512, 128, 512, 256, 512
PACK = 4
RUN = 8
GROUPS = 4
LIST_ROWS = 16
CHUNKS = (256, 128, 128)
GATE_BANKS, VALUE_BANKS, PAIR_BANKS = 3, 3, 2

FLOPS = 2 * K * H * S * 2 + 2 * H * N * U


def tile_picked_yfenw_add_p_kernel(
    tc, x_words, x_scales, w1, w2, st, lam, unit, w3, offs, m1, m2, out
):
    nc = tc.nc
    with ExitStack() as ctx:
        keep = ctx.enter_context(tc.tile_pool(name="keep", bufs=1))
        psum = ctx.enter_context(tc.psum_pool(name="psum", bufs=1))

        def tile(shape, dtype, name, after=None):
            return keep.tile(shape, dtype, name=name, tag=after or name, align_bytes=64)

        def dealt_rows(src, t):
            return src.rearrange("(b t r) c -> t b r c", t=PACK, r=RUN)[t]

        offs_sb = keep.tile([P, S // LIST_ROWS], U16, name="offs_sb")
        m1_sb = keep.tile([P, U // LIST_ROWS], U16, name="m1_sb")
        m2_sb = keep.tile([P, U // LIST_ROWS], U16, name="m2_sb")
        table_words = tile([P, T], I32, "table_words")
        table_scales = tile([P, T], U8, "table_scales")
        w2_raw = tile([P, PACK, H], F32, "w2_raw")
        w1_raw = tile([P, PACK, H], F32, "w1_raw")
        unit_rows = tile([P, P], F32, "unit_rows")
        unit_sb = tile([P, PACK], F32, "unit_sb")
        st_sb = [tile([P, U], F32, "st%d" % t) for t in range(PACK)]
        lam_sb = [tile([P, U], F32, "lam%d" % t) for t in range(PACK)]
        w3_raw = tile([P, PACK, N], F32, "w3_raw")

        nc.gpsimd.memset(table_scales[:].bitcast(I32), 0)
        nc.vector.memset(unit_rows[:], 0.0)

        w2_rows = w2.rearrange("(p j) c -> p j c", j=PACK)
        nc.sync.dma_start(w2_raw[:, 0:2, :], w2_rows[:, 0:2, :])
        for q in range(4):
            nc.sync.dma_start(
                table_scales[32 * q : 32 * q + 4, :].bitcast(I32), x_scales[0, 4 * q : 4 * q + 4, :].bitcast(I32)
            )
        nc.sync.dma_start(offs_sb[:], offs)
        nc.sync.dma_start(table_words[:], x_words[0].rearrange("p c r -> p (c r)").bitcast(I32))
        nc.sync.dma_start(w2_raw[:, 2:4, :], w2_rows[:, 2:4, :])
        nc.sync.dma_start(w1_raw[:], w1.rearrange("(p j) c -> p j c", j=PACK))
        nc.sync.dma_start(unit_rows[0:PACK, :], unit.rearrange("(b t r) o -> t b (r o)", t=PACK, r=RUN))
        nc.sync.dma_start(m1_sb[:], m1)
        nc.sync.dma_start(st_sb[0][:], dealt_rows(st, 0))
        for t in range(PACK):
            if t + 1 < PACK:
                nc.sync.dma_start(st_sb[t + 1][:], dealt_rows(st, t + 1))
            nc.sync.dma_start(lam_sb[t][:], dealt_rows(lam, t))
            if t == 0:
                nc.sync.dma_start(m2_sb[:], m2)
        for t in range(PACK):
            nc.sync.dma_start(w3_raw[:, t, :], dealt_rows(w3, t))

        ident = tile([P, P], F32, "ident")
        warm = tile([P, 1], F32, "warm")
        nc.gpsimd.memset(ident[:], 0.0)
        nc.scalar.activation(warm[:], ident[:, 0:1], SIGMOID)
        make_identity(nc, ident[:], nomemset=True)

        words = tile([P, S], U32, "words")
        picked_scales = tile([P, S], U8, "picked_scales")
        scales = tile([P, S], U8, "scales")
        nc.vector.tensor_copy(picked_scales[:], table_scales[:].indirect(offs_sb[:]))
        nc.vector.tensor_copy(
            scales[:].rearrange("p (d v) -> p d v", d=2), picked_scales[:].rearrange("p (v d) -> p d v", d=2)
        )
        nc.vector.tensor_copy(
            words[:].rearrange("p (d v) -> p v d", d=2), table_words[:].bitcast(U32).indirect(offs_sb[:])
        )

        def copy_on(on_vector, dst, src):
            if on_vector:
                nc.vector.tensor_copy(dst, src)
            else:
                nc.scalar.copy(dst, src)

        def weave_weights(raw, t, name, on_vector):
            woven = tile([P, P * PACK], BF16, name)
            dst = woven[:].rearrange("p (b r j) -> p b j r", r=RUN, j=PACK)
            src = raw[:].rearrange("p j (b t r) -> p t b j r", t=PACK, r=RUN)[:, t]
            copy_on(on_vector, dst, src)
            return woven

        def quantise(woven, columns, name):
            codes = tile([P, columns], U32, name + "_codes")
            planes = tile([P, columns], U8, name + "_scales")
            nc.vector.quantize_mx(out=codes[:].bitcast(FP8X4), scales=planes[:], in_=woven[:])
            return codes, planes

        def product(quantised, tag, bufs):
            codes, planes = quantised
            bank = psum.tile([P, GROUPS, P], F32, name="bank_" + tag, tag=tag, bufs=bufs)
            for a in range(GROUPS):
                tokens = slice(a * P, (a + 1) * P)
                nc.tensor.matmul_mx(
                    out=bank[:, a, :],
                    lhsT=words[:, tokens].bitcast(FP8X4),
                    lhsT_scale=scales[:, tokens],
                    rhs=codes[:].bitcast(FP8X4),
                    rhs_scale=planes[:],
                    start=True,
                    stop=True,
                )
            return bank

        window = [tile([P, V + S], F32, "window%d" % t) for t in range(PACK)]
        gated = [tile([P, GROUPS, P], F32, "gated%d" % t) for t in range(PACK)]
        lv2 = [tile([P, U], F32, "lv2_%d" % t) for t in range(PACK)]
        lw = [tile([P, U], F32, "lw%d" % t) for t in range(PACK)]
        st_scaled = {}
        st_scaled_after = (None, "gated0", "gated1", "gated2")

        def gate(t, bank):
            nc.scalar.activation(window[t][:, V:], bank[:].rearrange("p a f -> p (a f)"), SIGMOID)

        def apply_gate(t, bank):
            nc.vector.tensor_tensor(
                gated[t][:].rearrange("p a f -> p (a f)"), bank[:].rearrange("p a f -> p (a f)"), window[t][:, V:], MULT
            )

        def pair_sum(t):
            bank = psum.tile([P, V], F32, name="bank_pair", tag="pair", bufs=PAIR_BANKS)
            for h in range(2):
                for d in range(2):
                    nc.tensor.matmul(
                        bank[:, h * P : (h + 1) * P],
                        lhsT=gated[t][:, 2 * d + h, :],
                        rhs=ident[:],
                        is_transpose=True,
                        start=(d == 0),
                        stop=(d == 1),
                    )
            nc.scalar.activation(window[t][:, 0:V], bank[:], COPY, scale=unit_sb[:, t : t + 1])

        def scale_st(t):
            st_scaled[t] = tile([P, U], F32, "st_scaled%d" % t, st_scaled_after[t])
            nc.scalar.activation(st_scaled[t][:], st_sb[t][:], COPY, scale=unit_sb[:, t : t + 1])

        def look_up_pairs(t):
            nc.vector.tensor_tensor(lv2[t][:], window[t][:].indirect(m1_sb[:]), st_scaled[t][:], ADD)

        def weigh(t):
            nc.vector.tensor_tensor(lw[t][:], lv2[t][:], lam_sb[t][:], MULT)

        w2_woven = [weave_weights(w2_raw, t, "w2_woven%d" % t, t == PACK - 1) for t in range(PACK)]
        w2q = [quantise(w2_woven[t], P, "w2_%d" % t) for t in range(PACK)]
        gate_banks = [product(w2q[t], "gate", GATE_BANKS) for t in range(GATE_BANKS)]
        gate(0, gate_banks[0])
        gate_banks.append(product(w2q[3], "gate", GATE_BANKS))
        for t in range(1, PACK):
            gate(t, gate_banks[t])
        unit_bank = psum.tile([P, P], F32, name="unit_bank", tag="gate", bufs=GATE_BANKS)
        nc.tensor.transpose(unit_bank[:], unit_rows[:], ident[:])
        nc.scalar.copy(unit_sb[:], unit_bank[:, 0:PACK])

        w1_woven = [weave_weights(w1_raw, t, "w1_woven%d" % t, True) for t in (0, 1)]
        w1q = [quantise(w1_woven[t], P, "w1_%d" % t) for t in (0, 1)]
        w1_woven.append(weave_weights(w1_raw, 2, "w1_woven2", False))
        value_banks = [product(w1q[t], "value", VALUE_BANKS) for t in (0, 1)]
        apply_gate(0, value_banks[0])
        apply_gate(1, value_banks[1])
        scale_st(0)
        pair_sum(0)
        value_banks.append(product(quantise(w1_woven[2], P, "w1_2"), "value", VALUE_BANKS))
        w1_woven.append(weave_weights(w1_raw, 3, "w1_woven3", False))
        pair_sum(1)
        scale_st(1)
        look_up_pairs(0)
        value_banks.append(product(quantise(w1_woven[3], P, "w1_3"), "value", VALUE_BANKS))
        apply_gate(2, value_banks[2])
        pair_sum(2)
        scale_st(2)
        look_up_pairs(1)
        apply_gate(3, value_banks[3])
        pair_sum(3)
        scale_st(3)
        weigh(0)
        look_up_pairs(2)
        weigh(1)
        look_up_pairs(3)
        weigh(2)

        def weave_rows(dst, src, on_vector):
            copy_on(
                on_vector,
                dst.rearrange("p (g i t) -> p g t i", i=4, t=PACK),
                src.rearrange("p t (g i) -> p g t i", i=4),
            )

        w3_woven = tile([P, N * PACK], BF16, "w3_woven", "gated3")
        weave_rows(w3_woven[:], w3_raw[:], False)

        starts = [sum(CHUNKS[:c]) for c in range(len(CHUNKS))]
        last = len(CHUNKS) - 1
        hid = {}
        hid_woven = [tile([P, PACK * width], BF16, "hid_woven%d" % c) for c, width in enumerate(CHUNKS)]

        def look_up_nodes(c, t):
            c0, width = starts[c], CHUNKS[c]
            if t == 0:
                hid[c] = tile([P, PACK, width], F32, "hid%d" % c, "hid%d" % (c % 2))
            offsets = m2_sb[:, c0 // LIST_ROWS : (c0 + width) // LIST_ROWS]
            nc.vector.tensor_tensor(hid[c][:, t, :], lv2[t][:].indirect(offsets), lw[t][:, c0 : c0 + width], ADD)

        def project(c):
            c0, width = starts[c], CHUNKS[c]
            codes, planes = quantise(hid_woven[c], width, "hid_%d" % c)
            bank = psum.tile([P, width], F32, name="bank_out", tag="gate", bufs=GATE_BANKS)
            nc.tensor.matmul_mx(
                out=bank[:],
                lhsT=w3_codes[:].bitcast(FP8X4),
                lhsT_scale=w3_scales[:],
                rhs=codes[:].bitcast(FP8X4),
                rhs_scale=planes[:],
                start=True,
                stop=True,
            )
            result = tile([P, width], F32, "result%d" % c)
            copy_on(c == last, result[:], bank[:])
            nc.sync.dma_start(out[:, c0 : c0 + width], result[:])

        look_up_nodes(0, 0)
        weigh(3)
        w3_codes, w3_scales = quantise(w3_woven, N, "w3")
        for t in range(1, PACK):
            look_up_nodes(0, t)
        weave_rows(hid_woven[0][:], hid[0][:], False)
        for t in range(PACK):
            look_up_nodes(1, t)
        weave_rows(hid_woven[1][:], hid[1][:], False)
        project(0)
        for t in range(PACK):
            look_up_nodes(2, t)
        weave_rows(hid_woven[2][:], hid[2][:], True)
        project(1)
        project(2)
